import numpy as np
import ml_dtypes


def mxq(x, axis, fmt="e4m3"):
    dtype, down = {"e4m3": (ml_dtypes.float8_e4m3fn, 7), "e5m2": (ml_dtypes.float8_e5m2, 14)}[fmt]
    v = np.moveaxis(np.asarray(x, np.float32).astype(ml_dtypes.bfloat16).astype(np.float64), axis, -1)
    blocks = v.reshape(v.shape[:-1] + (-1, 32))
    amax = np.abs(blocks).max(-1, keepdims=True)
    byte = np.maximum(np.where(amax > 0, np.frexp(amax)[1] - 1 + 127, 0) - down, 1)
    scale = np.exp2(byte - 127.0)
    codes = (blocks / scale).astype(np.float32).astype(dtype).astype(np.float64)
    return np.moveaxis((codes * scale).reshape(v.shape), -1, axis)


WIDE = False


def mx_kscale(k):
    if not WIDE:
        return np.ones(k)
    levels = np.array([30, -30])
    if k % 512:
        return np.exp2(np.random.permutation(np.resize(levels, k // 32))).repeat(32)
    a = np.empty((k // 512, 16))
    for p in range(k // 512):
        a[p, :8] = np.random.permutation(np.resize(levels, 8))
        for g in range(8):
            far = levels[np.abs(levels - a[p, g]) >= 10]
            a[p, g + 8] = far[np.random.randint(len(far))]
    return np.exp2(a.ravel()).repeat(32)


def f64(x):
    return np.asarray(x).astype(np.float64)


def striped(idx):
    return np.tile(np.asarray(idx).reshape(-1, 16).T, (8, 1)).astype(np.uint16)


def unstriped(offs):
    return offs[:16].T.reshape(-1).astype(np.int64)


E2M1 = np.array([0.0, 0.5, 1.0, 1.5, 2.0, 3.0, 4.0, 6.0, -0.0, -0.5, -1.0, -1.5, -2.0, -3.0, -4.0, -6.0])


def pack_weight(w, fmt):
    k, n = w.shape
    w = f64(np.asarray(w, np.float32).astype(ml_dtypes.bfloat16)).reshape(k // 32, 32, n)
    amax = np.abs(w).max(1)
    if fmt in ("e4m3", "e5m2"):
        byte = np.frexp(amax)[1] - 1 + 127 - (7 if fmt == "e4m3" else 14)
    else:
        mant, ex = np.frexp(amax / 6.0)
        byte = np.where(mant > 0.5, ex, ex - 1) + 127
    byte = np.clip(np.where(amax > 0, byte, 1), 1, 254)
    scaled = (w * np.exp2(127.0 - byte)[:, None, :]).reshape(k, n).astype(np.float32)
    by_word = np.ascontiguousarray(scaled.reshape(k // 512, 128, 4, n).transpose(0, 1, 3, 2))
    if fmt in ("e4m3", "e5m2"):
        words = by_word.astype(ml_dtypes.float8_e4m3fn if fmt == "e4m3" else ml_dtypes.float8_e5m2).view(np.uint8)
    else:
        c = by_word.astype(ml_dtypes.float4_e2m1fn).view(np.uint8) & 0xF
        words = (c[..., 0::2] | (c[..., 1::2] << 4)).reshape(k // 512, 128, 2 * n)
    return np.ascontiguousarray(words), np.ascontiguousarray(byte.astype(np.uint8).reshape(k // 512, 16, n))


def unpack_weight(words, scales, fmt):
    g, _, n = scales.shape
    words = np.ascontiguousarray(words).reshape(g, 128, n, -1)
    if fmt in ("e4m3", "e5m2"):
        vals = words.view(ml_dtypes.float8_e4m3fn if fmt == "e4m3" else ml_dtypes.float8_e5m2).astype(np.float64)
    else:
        nib = np.empty((g, 128, n, 4), np.uint8)
        nib[..., 0::2] = words & 0xF
        nib[..., 1::2] = words >> 4
        vals = E2M1[nib]
    vals = vals * np.repeat(np.exp2(scales.astype(np.float64) - 127.0), 8, axis=1)[..., None]
    return vals.transpose(0, 1, 3, 2).reshape(g * 512, n)


def sigmoid(v):
    return 1.0 / (1.0 + np.exp(-v))


K, T, J, R, C, Q, N, S = 512, 1024, 256, 512, 512, 1024, 256, 1024


def setup_inputs():
    n = np.random.standard_normal
    idx = np.random.permutation(T)[:J]
    idx2 = np.random.permutation(C)[:J]
    idx3 = np.random.permutation(C)[:J]
    idx4 = np.random.permutation(Q)[:J]
    idx5 = np.random.permutation(S)[:N]
    fk = mx_kscale(K)
    fr = mx_kscale(R)
    xtp = pack_weight(n((K, T)) / fk[:, None], "e5m2")
    wp = pack_weight(n((K, R)) * 1 / np.sqrt(K) * fk[:, None] * fr, "e2m1")
    w2p = pack_weight(n((K, R)) * 1 / np.sqrt(K) * fk[:, None] * fr, "e4m3")
    vsp = pack_weight(n((R, S)) * 1 / np.sqrt(R) / fr[:, None], "e2m1")
    return {
        "xt_words": xtp[0],
        "xt_scales": xtp[1],
        "w_words": wp[0],
        "w_scales": wp[1],
        "w2_words": w2p[0],
        "w2_scales": w2p[1],
        "tg": (1.0 * n((R, Q))).astype(np.float32),
        "sg": (np.random.uniform(0.6, 1.6, (R, 1))).astype(np.float32),
        "bg": (np.random.uniform(-1.0, 1.0, (R, 1))).astype(np.float32),
        "vs_words": vsp[0],
        "vs_scales": vsp[1],
        "offs": striped(idx),
        "offs2": striped(idx2),
        "offs3": striped(idx3),
        "offs4": striped(idx4),
        "offs5": striped(idx5),
    }


def reference(xt_words, xt_scales, w_words, w_scales, w2_words, w2_scales, tg, sg, bg, vs_words, vs_scales, offs, offs2, offs3, offs4, offs5):
    idx = unstriped(offs)
    idx2 = unstriped(offs2)
    idx3 = unstriped(offs3)
    idx4 = unstriped(offs4)
    idx5 = unstriped(offs5)
    xtu = unpack_weight(xt_words, xt_scales, "e5m2")
    wu = unpack_weight(w_words, w_scales, "e2m1")
    w2u = unpack_weight(w2_words, w2_scales, "e4m3")
    vsu = unpack_weight(vs_words, vs_scales, "e2m1")
    xtidxg = xtu[:, idx]
    a = wu.T @ xtidxg
    b = w2u.T @ xtidxg
    pw = np.zeros((R, C))
    pw[:, idx2] = a
    hid = np.maximum(pw[:, idx3], b) * sigmoid(f64(tg)[:, idx4] * f64(sg) + f64(bg))
    vsidx5g = vsu[:, idx5]
    hidq = mxq(hid, 0, "e4m3")
    y = vsidx5g.T @ hidq
    return y

@@ -1,0 +1,195 @@
+from contextlib import ExitStack
+
+import concourse.mybir as mybir
+
+K, T, J, R, C, Q, N, S = 512, 1024, 256, 512, 512, 1024, 256, 1024
+FLOPS = 2 * K * R * J * 2 + 2 * R * N * J
+
+F32 = mybir.dt.float32
+BF16 = mybir.dt.bfloat16
+I32 = mybir.dt.int32
+U32 = mybir.dt.uint32
+U16 = mybir.dt.uint16
+U8 = mybir.dt.uint8
+E4M3 = mybir.dt.float8_e4m3fn_x4
+E5M2 = mybir.dt.float8_e5m2_x4
+E2M1 = mybir.dt.float4_e2m1fn_x4
+ACT = mybir.ActivationFunctionType
+ALU = mybir.AluOpType
+
+P = 128
+PACK = 4
+
+
+def tile_list_boardtable_twow_store_plain_kernel(
+    tc, xt_words, xt_scales, w_words, w_scales, w2_words, w2_scales, tg, sg, bg,
+    vs_words, vs_scales, offs, offs2, offs3, offs4, offs5, out,
+):
+    nc = tc.nc
+    with ExitStack() as ctx:
+        lists = ctx.enter_context(tc.tile_pool(name="lists", bufs=1))
+        keep = ctx.enter_context(tc.tile_pool(name="keep", bufs=1))
+        psum = ctx.enter_context(tc.psum_pool(name="psum", bufs=1))
+
+        def load_list(src, name):
+            tile = lists.tile([P, J // 16], U16, name=name)
+            nc.sync.dma_start(tile[:], src)
+            return tile
+
+        def zero_plane(width, name):
+            plane = keep.tile([P, width], U8, name=name, align_bytes=64)
+            nc.vector.memset(plane[:].bitcast(I32), 0)
+            return plane
+
+        def load_plane(queues, plane, src):
+            for q in range(4):
+                queues[q].dma_start(
+                    out=plane[32 * q : 32 * q + 4, :].bitcast(I32),
+                    in_=src[0, 4 * q : 4 * q + 4, :].bitcast(I32),
+                )
+
+        def load_words(queue, src, width, dtype, name):
+            tile = keep.tile([P, width], dtype, name=name, align_bytes=64)
+            queue.dma_start(out=tile[:].bitcast(I32), in_=src.bitcast(I32))
+            return tile
+
+        tg_rows = tg.rearrange("(p t) q -> p t q", t=PACK)
+
+        def load_gate(t):
+            tile = keep.tile([P, Q], F32, name="gate%d" % t, align_bytes=64)
+            nc.sync.dma_start(out=tile[:], in_=tg_rows[:, t, :])
+            return tile
+
+        xs = zero_plane(T, "xs")
+        ws = zero_plane(R, "ws")
+        vsc = zero_plane(S, "vsc")
+        w2s = zero_plane(R, "w2s")
+        on_sync = [nc.sync] * 4
+        tok = load_list(offs, "tok")
+        xw = load_words(nc.sync, xt_words[0].rearrange("p c b -> p (c b)"), T, U32, "xw")
+        ww = load_words(nc.sync, w_words[0], R, U16, "ww")
+        load_plane(on_sync, xs, xt_scales)
+        load_plane(on_sync, ws, w_scales)
+        load_plane([nc.gpsimd] * 4, vsc, vs_scales)
+        gate = [load_gate(0)]
+        put = load_list(offs2, "put")
+        slope = keep.tile([P, PACK], F32, name="slope")
+        nc.sync.dma_start(out=slope[:], in_=sg.rearrange("(p t) o -> p (t o)", t=PACK))
+        shift = keep.tile([P, PACK], F32, name="shift")
+        nc.sync.dma_start(out=shift[:], in_=bg.rearrange("(p t) o -> p (t o)", t=PACK))
+        look = load_list(offs4, "look")
+        w2w = load_words(nc.sync, w2_words[0].rearrange("p c b -> p (c b)"), R, U32, "w2w")
+        load_plane(on_sync, w2s, w2_scales)
+        gate.append(load_gate(1))
+        get = load_list(offs3, "get")
+        vw = load_words(nc.sync, vs_words[0], S, U16, "vw")
+        gate.append(load_gate(2))
+        entry = load_list(offs5, "entry")
+        gate.append(load_gate(3))
+
+        board = []
+        for t in range(PACK):
+            tile = keep.tile([P, C], F32, name="board%d" % t, align_bytes=64)
+            nc.vector.memset(tile[:], 0.0)
+            board.append(tile)
+
+        def deal(src, dtype, name):
+            dealt = keep.tile([P, PACK, P], dtype, name=name, align_bytes=64)
+            nc.vector.tensor_copy(
+                out=dealt[:].rearrange("p t m -> p m t"),
+                in_=src[:].rearrange("p (m t) -> p m t", t=PACK),
+            )
+            return dealt
+
+        def pick(src, offsets, dtype, name):
+            picked = keep.tile([P, J], dtype, name=name, align_bytes=64)
+            nc.vector.tensor_copy(out=picked[:], in_=src[:].indirect(offsets[:]))
+            return picked
+
+        xs_g = pick(xs, tok, U8, "xs_g")
+        ww_d = deal(ww, U16, "ww_d")
+        xw_g = pick(xw, tok, U32, "xw_g")
+        ws_d = deal(ws, U8, "ws_d")
+
+        sig = keep.tile([P, PACK, J], F32, name="sig", align_bytes=64)
+
+        def look_up_gate(t):
+            nc.scalar.activation(
+                out=sig[:, t, :], in_=gate[t][:].indirect(look[:]), func=ACT.Sigmoid,
+                bias=shift[:, t : t + 1], scale=slope[:, t : t + 1],
+            )
+
+        look_up_gate(0)
+
+        a_ps = []
+        for t in range(PACK):
+            acc = psum.tile([P, J], F32, name="a_ps%d" % t)
+            nc.tensor.matmul_mx(
+                out=acc[:], lhsT=ww_d[:, t, :].bitcast(E2M1), lhsT_scale=ws_d[:, t, :],
+                rhs=xw_g[:].bitcast(E5M2), rhs_scale=xs_g[:], start=True, stop=True,
+            )
+            a_ps.append(acc)
+
+        w2w_d = deal(w2w, U32, "w2w_d")
+        w2s_d = deal(w2s, U8, "w2s_d")
+        b_ps = []
+        for u in range(2):
+            acc = psum.tile([P, 2, J], F32, name="b_ps%d" % u)
+            for e in range(2):
+                t = 2 * u + e
+                nc.tensor.matmul_mx(
+                    out=acc[:, e, :], lhsT=w2w_d[:, t, :].bitcast(E4M3), lhsT_scale=w2s_d[:, t, :],
+                    rhs=xw_g[:].bitcast(E5M2), rhs_scale=xs_g[:], start=True, stop=True,
+                )
+            b_ps.append(acc)
+
+        for t in range(PACK):
+            a_sb = keep.tile([P, J], F32, name="a_sb%d" % t, align_bytes=64)
+            if t % 2 == 0:
+                nc.scalar.copy(out=a_sb[:], in_=a_ps[t][:])
+                nc.scalar.activation(out=board[t][:].indirect(put[:]), in_=a_sb[:], func=ACT.Copy)
+            else:
+                nc.vector.tensor_copy(out=a_sb[:], in_=a_ps[t][:])
+                nc.vector.tensor_copy(out=board[t][:].indirect(put[:]), in_=a_sb[:])
+
+        vw_g = pick(vw, entry, U16, "vw_g")
+        vs_g = pick(vsc, entry, U8, "vs_g")
+
+        larger = keep.tile([P, PACK, J], F32, name="larger", align_bytes=64)
+        hid = keep.tile([P, J, PACK], BF16, name="hid", align_bytes=64)
+        for u in range(2):
+            for e in range(2):
+                t = 2 * u + e
+                got = keep.tile([P, J], F32, name="got%d" % t, align_bytes=64)
+                nc.scalar.activation(out=got[:], in_=board[t][:].indirect(get[:]), func=ACT.Copy)
+                nc.vector.tensor_tensor(out=larger[:, t, :], in0=got[:], in1=b_ps[u][:, e, :], op=ALU.max)
+            for e in range(2):
+                t = 2 * u + e
+                if t > 0:
+                    look_up_gate(t)
+            pair = slice(2 * u, 2 * u + 2)
+            nc.vector.tensor_tensor(
+                out=hid[:, :, pair],
+                in0=larger[:, pair, :].rearrange("p t j -> p j t"),
+                in1=sig[:, pair, :].rearrange("p t j -> p j t"),
+                op=ALU.mult,
+            )
+
+        hid_w = keep.tile([P, J], U32, name="hid_w", align_bytes=64)
+        hid_s = keep.tile([P, J], U8, name="hid_s", align_bytes=64)
+        nc.vector.quantize_mx(out=hid_w[:].bitcast(E4M3), scales=hid_s[:], in_=hid[:].rearrange("p j t -> p (j t)"))
+
+        for h in range(2):
+            cols = slice(h * P, (h + 1) * P)
+            acc = psum.tile([P, J], F32, name="o_ps%d" % h)
+            nc.tensor.matmul_mx(
+                out=acc[:], lhsT=vw_g[:, cols].bitcast(E2M1), lhsT_scale=vs_g[:, cols],
+                rhs=hid_w[:].bitcast(E4M3), rhs_scale=hid_s[:], start=True, stop=True,
+            )
+            res = keep.tile([P, J], F32, name="res%d" % h, align_bytes=64)
+            if h == 0:
+                nc.scalar.copy(out=res[:], in_=acc[:])
+                nc.scalar.dma_start(out=out[cols, :], in_=res[:])
+            else:
+                nc.vector.tensor_copy(out=res[:], in_=acc[:])
+                nc.sync.dma_start(out=out[cols, :], in_=res[:])

@@ -29,6 +29,7 @@ def tile_list_boardtable_twow_store_plain_kernel(
     with ExitStack() as ctx:
         lists = ctx.enter_context(tc.tile_pool(name="lists", bufs=1))
         keep = ctx.enter_context(tc.tile_pool(name="keep", bufs=1))
+        ring = ctx.enter_context(tc.tile_pool(name="ring", bufs=2))
         psum = ctx.enter_context(tc.psum_pool(name="psum", bufs=1))
 
         def load_list(src, name):
@@ -41,9 +42,9 @@ def tile_list_boardtable_twow_store_plain_kernel(
             nc.vector.memset(plane[:].bitcast(I32), 0)
             return plane
 
-        def load_plane(queues, plane, src):
-            for q in range(4):
-                queues[q].dma_start(
+        def load_plane(plane, src, queue, quadrants):
+            for q in quadrants:
+                queue.dma_start(
                     out=plane[32 * q : 32 * q + 4, :].bitcast(I32),
                     in_=src[0, 4 * q : 4 * q + 4, :].bitcast(I32),
                 )
@@ -64,27 +65,27 @@ def tile_list_boardtable_twow_store_plain_kernel(
         ws = zero_plane(R, "ws")
         vsc = zero_plane(S, "vsc")
         w2s = zero_plane(R, "w2s")
-        on_sync = [nc.sync] * 4
         tok = load_list(offs, "tok")
-        xw = load_words(nc.sync, xt_words[0].rearrange("p c b -> p (c b)"), T, U32, "xw")
         ww = load_words(nc.sync, w_words[0], R, U16, "ww")
-        load_plane(on_sync, xs, xt_scales)
-        load_plane(on_sync, ws, w_scales)
-        load_plane([nc.gpsimd] * 4, vsc, vs_scales)
-        gate = [load_gate(0)]
+        xw = load_words(nc.sync, xt_words[0].rearrange("p c b -> p (c b)"), T, U32, "xw")
+        load_plane(xs, xt_scales, nc.sync, range(4))
+        load_plane(ws, w_scales, nc.sync, range(3))
+        load_plane(ws, w_scales, nc.gpsimd, range(3, 4))
+        w2w = load_words(nc.sync, w2_words[0].rearrange("p c b -> p (c b)"), R, U32, "w2w")
         put = load_list(offs2, "put")
+        load_plane(w2s, w2_scales, nc.sync, range(4))
+        get = load_list(offs3, "get")
+        vw = load_words(nc.sync, vs_words[0], S, U16, "vw")
+        entry = load_list(offs5, "entry")
+        gate = [load_gate(0)]
+        load_plane(vsc, vs_scales, nc.sync, range(4))
+        gate.append(load_gate(1))
+        look = load_list(offs4, "look")
         slope = keep.tile([P, PACK], F32, name="slope")
         nc.sync.dma_start(out=slope[:], in_=sg.rearrange("(p t) o -> p (t o)", t=PACK))
         shift = keep.tile([P, PACK], F32, name="shift")
         nc.sync.dma_start(out=shift[:], in_=bg.rearrange("(p t) o -> p (t o)", t=PACK))
-        look = load_list(offs4, "look")
-        w2w = load_words(nc.sync, w2_words[0].rearrange("p c b -> p (c b)"), R, U32, "w2w")
-        load_plane(on_sync, w2s, w2_scales)
-        gate.append(load_gate(1))
-        get = load_list(offs3, "get")
-        vw = load_words(nc.sync, vs_words[0], S, U16, "vw")
         gate.append(load_gate(2))
-        entry = load_list(offs5, "entry")
         gate.append(load_gate(3))
 
         board = []
@@ -93,11 +94,11 @@ def tile_list_boardtable_twow_store_plain_kernel(
             nc.vector.memset(tile[:], 0.0)
             board.append(tile)
 
-        def deal(src, dtype, name):
+        def deal(copy, src, dtype, name, run):
             dealt = keep.tile([P, PACK, P], dtype, name=name, align_bytes=64)
-            nc.vector.tensor_copy(
-                out=dealt[:].rearrange("p t m -> p m t"),
-                in_=src[:].rearrange("p (m t) -> p m t", t=PACK),
+            copy(
+                out=dealt[:].rearrange("p t (g i) -> p g t i", i=run),
+                in_=src[:].rearrange("p (g i t) -> p g t i", i=run, t=PACK),
             )
             return dealt
 
@@ -107,9 +108,9 @@ def tile_list_boardtable_twow_store_plain_kernel(
             return picked
 
         xs_g = pick(xs, tok, U8, "xs_g")
-        ww_d = deal(ww, U16, "ww_d")
+        ww_d = deal(nc.scalar.copy, ww, U16, "ww_d", 8)
         xw_g = pick(xw, tok, U32, "xw_g")
-        ws_d = deal(ws, U8, "ws_d")
+        ws_d = deal(nc.vector.tensor_copy, ws, U8, "ws_d", 16)
 
         sig = keep.tile([P, PACK, J], F32, name="sig", align_bytes=64)
 
@@ -119,19 +120,17 @@ def tile_list_boardtable_twow_store_plain_kernel(
                 bias=shift[:, t : t + 1], scale=slope[:, t : t + 1],
             )
 
-        look_up_gate(0)
-
-        a_ps = []
-        for t in range(PACK):
+        a_ps = {}
+        for t in (0, 1, 3, 2):
             acc = psum.tile([P, J], F32, name="a_ps%d" % t)
             nc.tensor.matmul_mx(
                 out=acc[:], lhsT=ww_d[:, t, :].bitcast(E2M1), lhsT_scale=ws_d[:, t, :],
                 rhs=xw_g[:].bitcast(E5M2), rhs_scale=xs_g[:], start=True, stop=True,
             )
-            a_ps.append(acc)
+            a_ps[t] = acc
 
-        w2w_d = deal(w2w, U32, "w2w_d")
-        w2s_d = deal(w2s, U8, "w2s_d")
+        w2w_d = deal(nc.vector.tensor_copy, w2w, U32, "w2w_d", 4)
+        w2s_d = deal(nc.vector.tensor_copy, w2s, U8, "w2s_d", 16)
         b_ps = []
         for u in range(2):
             acc = psum.tile([P, 2, J], F32, name="b_ps%d" % u)
@@ -143,53 +142,70 @@ def tile_list_boardtable_twow_store_plain_kernel(
                 )
             b_ps.append(acc)
 
-        for t in range(PACK):
-            a_sb = keep.tile([P, J], F32, name="a_sb%d" % t, align_bytes=64)
-            if t % 2 == 0:
-                nc.scalar.copy(out=a_sb[:], in_=a_ps[t][:])
-                nc.scalar.activation(out=board[t][:].indirect(put[:]), in_=a_sb[:], func=ACT.Copy)
+        a_sb = {}
+        for t in (0, 1, 3, 2):
+            a_sb[t] = keep.tile([P, J], F32, name="a_sb%d" % t, align_bytes=64)
+            if t == 2:
+                nc.scalar.copy(out=a_sb[t][:], in_=a_ps[t][:])
             else:
-                nc.vector.tensor_copy(out=a_sb[:], in_=a_ps[t][:])
-                nc.vector.tensor_copy(out=board[t][:].indirect(put[:]), in_=a_sb[:])
+                nc.vector.tensor_copy(out=a_sb[t][:], in_=a_ps[t][:])
+        for t in range(PACK):
+            if t < 3:
+                nc.scalar.activation(out=board[t][:].indirect(put[:]), in_=a_sb[t][:], func=ACT.Copy)
+            else:
+                nc.vector.tensor_copy(out=board[t][:].indirect(put[:]), in_=a_sb[t][:])
 
         vw_g = pick(vw, entry, U16, "vw_g")
         vs_g = pick(vsc, entry, U8, "vs_g")
 
         larger = keep.tile([P, PACK, J], F32, name="larger", align_bytes=64)
-        hid = keep.tile([P, J, PACK], BF16, name="hid", align_bytes=64)
-        for u in range(2):
-            for e in range(2):
-                t = 2 * u + e
-                got = keep.tile([P, J], F32, name="got%d" % t, align_bytes=64)
-                nc.scalar.activation(out=got[:], in_=board[t][:].indirect(get[:]), func=ACT.Copy)
-                nc.vector.tensor_tensor(out=larger[:, t, :], in0=got[:], in1=b_ps[u][:, e, :], op=ALU.max)
-            for e in range(2):
-                t = 2 * u + e
-                if t > 0:
-                    look_up_gate(t)
+        for t in (0, 3, 1, 2):
+            got = ring.tile([P, J], F32, name="got", align_bytes=64)
+            nc.vector.tensor_copy(out=got[:], in_=board[t][:].indirect(get[:]))
+            nc.vector.tensor_tensor(out=larger[:, t, :], in0=got[:], in1=b_ps[t // 2][:, t % 2, :], op=ALU.max)
+        for t in range(PACK):
+            look_up_gate(t)
+        pairs = keep.tile([P, 2, J, 2], BF16, name="pairs", align_bytes=64)
+
+        def gate_pair(u, slots):
             pair = slice(2 * u, 2 * u + 2)
             nc.vector.tensor_tensor(
-                out=hid[:, :, pair],
-                in0=larger[:, pair, :].rearrange("p t j -> p j t"),
-                in1=sig[:, pair, :].rearrange("p t j -> p j t"),
+                out=pairs[:, u, slots, :],
+                in0=larger[:, pair, slots].rearrange("p t j -> p j t"),
+                in1=sig[:, pair, slots].rearrange("p t j -> p j t"),
                 op=ALU.mult,
             )
 
-        hid_w = keep.tile([P, J], U32, name="hid_w", align_bytes=64)
-        hid_s = keep.tile([P, J], U8, name="hid_s", align_bytes=64)
-        nc.vector.quantize_mx(out=hid_w[:].bitcast(E4M3), scales=hid_s[:], in_=hid[:].rearrange("p j t -> p (j t)"))
-
-        for h in range(2):
-            cols = slice(h * P, (h + 1) * P)
-            acc = psum.tile([P, J], F32, name="o_ps%d" % h)
-            nc.tensor.matmul_mx(
-                out=acc[:], lhsT=vw_g[:, cols].bitcast(E2M1), lhsT_scale=vs_g[:, cols],
-                rhs=hid_w[:].bitcast(E4M3), rhs_scale=hid_s[:], start=True, stop=True,
+        halves = [slice(g * P, (g + 1) * P) for g in range(2)]
+        gate_pair(0, slice(0, J))
+        for slots in halves:
+            gate_pair(1, slots)
+        pair_words = pairs[:].rearrange("p u j e -> p (u j e)").bitcast(I32).rearrange("p (u j) -> p j u", u=2)
+        hid = []
+        for g in range(2):
+            tile = keep.tile([P, P, PACK], BF16, name="hid%d" % g, align_bytes=64)
+            nc.vector.tensor_copy(
+                out=tile[:].rearrange("p j t -> p (j t)").bitcast(I32).rearrange("p (j u) -> p j u", u=2),
+                in_=pair_words[:, halves[g], :],
             )
-            res = keep.tile([P, J], F32, name="res%d" % h, align_bytes=64)
-            if h == 0:
+            hid.append(tile)
+        for g in range(2):
+            hid_w = keep.tile([P, P], U32, name="hid_w%d" % g, align_bytes=64)
+            hid_s = keep.tile([P, P], U8, name="hid_s%d" % g, align_bytes=64)
+            nc.vector.quantize_mx(
+                out=hid_w[:].bitcast(E4M3), scales=hid_s[:], in_=hid[g][:].rearrange("p j t -> p (j t)")
+            )
+            acc = psum.tile([P, 2, P], F32, name="o_ps%d" % g)
+            for h in range(2):
+                nc.tensor.matmul_mx(
+                    out=acc[:, h, :], lhsT=vw_g[:, halves[h]].bitcast(E2M1), lhsT_scale=vs_g[:, halves[h]],
+                    rhs=hid_w[:].bitcast(E4M3), rhs_scale=hid_s[:], start=True, stop=True,
+                )
+            res = keep.tile([P, 2, P], F32, name="res%d" % g, align_bytes=64)
+            dst = out[:, halves[g]].rearrange("(h p) j -> p h j", h=2)
+            if g == 0:
                 nc.scalar.copy(out=res[:], in_=acc[:])
-                nc.scalar.dma_start(out=out[cols, :], in_=res[:])
+                nc.scalar.dma_start(out=dst, in_=res[:])
             else:
                 nc.vector.tensor_copy(out=res[:], in_=acc[:])
-                nc.sync.dma_start(out=out[cols, :], in_=res[:])
+                nc.sync.dma_start(out=dst, in_=res[:])

@@ -67,31 +67,30 @@ def tile_list_boardtable_twow_store_plain_kernel(
         w2s = zero_plane(R, "w2s")
         tok = load_list(offs, "tok")
         ww = load_words(nc.sync, w_words[0], R, U16, "ww")
-        xw = load_words(nc.sync, xt_words[0].rearrange("p c b -> p (c b)"), T, U32, "xw")
-        load_plane(xs, xt_scales, nc.sync, range(4))
-        load_plane(ws, w_scales, nc.sync, range(3))
-        load_plane(ws, w_scales, nc.gpsimd, range(3, 4))
-        w2w = load_words(nc.sync, w2_words[0].rearrange("p c b -> p (c b)"), R, U32, "w2w")
         put = load_list(offs2, "put")
-        load_plane(w2s, w2_scales, nc.sync, range(4))
-        get = load_list(offs3, "get")
-        vw = load_words(nc.sync, vs_words[0], S, U16, "vw")
-        entry = load_list(offs5, "entry")
+        load_plane(xs, xt_scales, nc.sync, range(4))
+        xw = load_words(nc.sync, xt_words[0].rearrange("p c b -> p (c b)"), T, U32, "xw")
+        load_plane(ws, w_scales, nc.sync, range(4))
         gate = [load_gate(0)]
-        load_plane(vsc, vs_scales, nc.sync, range(4))
-        gate.append(load_gate(1))
         look = load_list(offs4, "look")
         slope = keep.tile([P, PACK], F32, name="slope")
         nc.sync.dma_start(out=slope[:], in_=sg.rearrange("(p t) o -> p (t o)", t=PACK))
         shift = keep.tile([P, PACK], F32, name="shift")
-        nc.sync.dma_start(out=shift[:], in_=bg.rearrange("(p t) o -> p (t o)", t=PACK))
+        nc.gpsimd.dma_start(out=shift[:], in_=bg.rearrange("(p t) o -> p (t o)", t=PACK))
+        w2w = load_words(nc.sync, w2_words[0].rearrange("p c b -> p (c b)"), R, U32, "w2w")
+        load_plane(w2s, w2_scales, nc.sync, range(4))
+        get = load_list(offs3, "get")
+        vw = load_words(nc.sync, vs_words[0], S, U16, "vw")
+        entry = load_list(offs5, "entry")
+        gate.append(load_gate(1))
+        load_plane(vsc, vs_scales, nc.sync, range(4))
         gate.append(load_gate(2))
         gate.append(load_gate(3))
 
         board = []
         for t in range(PACK):
             tile = keep.tile([P, C], F32, name="board%d" % t, align_bytes=64)
-            nc.vector.memset(tile[:], 0.0)
+            nc.gpsimd.memset(tile[:], 0.0)
             board.append(tile)
 
         def deal(copy, src, dtype, name, run):
@@ -120,8 +119,10 @@ def tile_list_boardtable_twow_store_plain_kernel(
                 bias=shift[:, t : t + 1], scale=slope[:, t : t + 1],
             )
 
+        look_up_gate(0)
+
         a_ps = {}
-        for t in (0, 1, 3, 2):
+        for t in (0, 3, 1, 2):
             acc = psum.tile([P, J], F32, name="a_ps%d" % t)
             nc.tensor.matmul_mx(
                 out=acc[:], lhsT=ww_d[:, t, :].bitcast(E2M1), lhsT_scale=ws_d[:, t, :],
@@ -142,70 +143,57 @@ def tile_list_boardtable_twow_store_plain_kernel(
                 )
             b_ps.append(acc)
 
-        a_sb = {}
-        for t in (0, 1, 3, 2):
-            a_sb[t] = keep.tile([P, J], F32, name="a_sb%d" % t, align_bytes=64)
-            if t == 2:
-                nc.scalar.copy(out=a_sb[t][:], in_=a_ps[t][:])
-            else:
-                nc.vector.tensor_copy(out=a_sb[t][:], in_=a_ps[t][:])
-        for t in range(PACK):
+        for t in (0, 3, 1, 2):
+            a_sb = keep.tile([P, J], F32, name="a_sb%d" % t, align_bytes=64)
+            nc.vector.tensor_copy(out=a_sb[:], in_=a_ps[t][:])
             if t < 3:
-                nc.scalar.activation(out=board[t][:].indirect(put[:]), in_=a_sb[t][:], func=ACT.Copy)
+                nc.scalar.activation(out=board[t][:].indirect(put[:]), in_=a_sb[:], func=ACT.Copy)
             else:
-                nc.vector.tensor_copy(out=board[t][:].indirect(put[:]), in_=a_sb[t][:])
+                nc.vector.tensor_copy(out=board[t][:].indirect(put[:]), in_=a_sb[:])
 
         vw_g = pick(vw, entry, U16, "vw_g")
         vs_g = pick(vsc, entry, U8, "vs_g")
 
         larger = keep.tile([P, PACK, J], F32, name="larger", align_bytes=64)
-        for t in (0, 3, 1, 2):
+        for t in (3, 0, 1, 2):
             got = ring.tile([P, J], F32, name="got", align_bytes=64)
             nc.vector.tensor_copy(out=got[:], in_=board[t][:].indirect(get[:]))
             nc.vector.tensor_tensor(out=larger[:, t, :], in0=got[:], in1=b_ps[t // 2][:, t % 2, :], op=ALU.max)
-        for t in range(PACK):
+        for t in range(1, PACK):
             look_up_gate(t)
-        pairs = keep.tile([P, 2, J, 2], BF16, name="pairs", align_bytes=64)
+        halves = [slice(g * P, (g + 1) * P) for g in range(2)]
+        hid = keep.tile([P, J, PACK], BF16, name="hid", align_bytes=64)
 
         def gate_pair(u, slots):
             pair = slice(2 * u, 2 * u + 2)
             nc.vector.tensor_tensor(
-                out=pairs[:, u, slots, :],
+                out=hid[:, slots, pair],
                 in0=larger[:, pair, slots].rearrange("p t j -> p j t"),
                 in1=sig[:, pair, slots].rearrange("p t j -> p j t"),
                 op=ALU.mult,
             )
 
-        halves = [slice(g * P, (g + 1) * P) for g in range(2)]
         gate_pair(0, slice(0, J))
         for slots in halves:
             gate_pair(1, slots)
-        pair_words = pairs[:].rearrange("p u j e -> p (u j e)").bitcast(I32).rearrange("p (u j) -> p j u", u=2)
-        hid = []
-        for g in range(2):
-            tile = keep.tile([P, P, PACK], BF16, name="hid%d" % g, align_bytes=64)
-            nc.vector.tensor_copy(
-                out=tile[:].rearrange("p j t -> p (j t)").bitcast(I32).rearrange("p (j u) -> p j u", u=2),
-                in_=pair_words[:, halves[g], :],
-            )
-            hid.append(tile)
         for g in range(2):
             hid_w = keep.tile([P, P], U32, name="hid_w%d" % g, align_bytes=64)
             hid_s = keep.tile([P, P], U8, name="hid_s%d" % g, align_bytes=64)
             nc.vector.quantize_mx(
-                out=hid_w[:].bitcast(E4M3), scales=hid_s[:], in_=hid[g][:].rearrange("p j t -> p (j t)")
+                out=hid_w[:].bitcast(E4M3), scales=hid_s[:],
+                in_=hid[:, halves[g], :].rearrange("p j t -> p (j t)"),
             )
-            acc = psum.tile([P, 2, P], F32, name="o_ps%d" % g)
             for h in range(2):
+                acc = psum.tile([P, P], F32, name="a_ps%d" % (2 * g + h))
                 nc.tensor.matmul_mx(
-                    out=acc[:, h, :], lhsT=vw_g[:, halves[h]].bitcast(E2M1), lhsT_scale=vs_g[:, halves[h]],
+                    out=acc[:], lhsT=vw_g[:, halves[h]].bitcast(E2M1), lhsT_scale=vs_g[:, halves[h]],
                     rhs=hid_w[:].bitcast(E4M3), rhs_scale=hid_s[:], start=True, stop=True,
                 )
-            res = keep.tile([P, 2, P], F32, name="res%d" % g, align_bytes=64)
-            dst = out[:, halves[g]].rearrange("(h p) j -> p h j", h=2)
-            if g == 0:
-                nc.scalar.copy(out=res[:], in_=acc[:])
-                nc.scalar.dma_start(out=dst, in_=res[:])
-            else:
-                nc.vector.tensor_copy(out=res[:], in_=acc[:])
-                nc.sync.dma_start(out=dst, in_=res[:])
+                res = keep.tile([P, P], F32, name="res%d" % (2 * g + h), align_bytes=64)
+                last = g == 1 and h == 1
+                if last:
+                    nc.vector.tensor_copy(out=res[:], in_=acc[:])
+                else:
+                    nc.scalar.copy(out=res[:], in_=acc[:])
+                queue = nc.scalar if (g == 1 and h == 0) else nc.sync
+                queue.dma_start(out=out[halves[h], halves[g]], in_=res[:])

from contextlib import ExitStack

import concourse.mybir as mybir

K, T, J, R, C, Q, N, S = 512, 1024, 256, 512, 512, 1024, 256, 1024
FLOPS = 2 * K * R * J * 2 + 2 * R * N * J

F32 = mybir.dt.float32
BF16 = mybir.dt.bfloat16
I32 = mybir.dt.int32
U32 = mybir.dt.uint32
U16 = mybir.dt.uint16
U8 = mybir.dt.uint8
E4M3 = mybir.dt.float8_e4m3fn_x4
E5M2 = mybir.dt.float8_e5m2_x4
E2M1 = mybir.dt.float4_e2m1fn_x4
ACT = mybir.ActivationFunctionType
ALU = mybir.AluOpType

P = 128
PACK = 4


def tile_list_boardtable_twow_store_plain_kernel(
    tc, xt_words, xt_scales, w_words, w_scales, w2_words, w2_scales, tg, sg, bg,
    vs_words, vs_scales, offs, offs2, offs3, offs4, offs5, out,
):
    nc = tc.nc
    with ExitStack() as ctx:
        lists = ctx.enter_context(tc.tile_pool(name="lists", bufs=1))
        keep = ctx.enter_context(tc.tile_pool(name="keep", bufs=1))
        ring = ctx.enter_context(tc.tile_pool(name="ring", bufs=2))
        psum = ctx.enter_context(tc.psum_pool(name="psum", bufs=1))

        def load_list(src, name):
            tile = lists.tile([P, J // 16], U16, name=name)
            nc.sync.dma_start(tile[:], src)
            return tile

        def zero_plane(width, name):
            plane = keep.tile([P, width], U8, name=name, align_bytes=64)
            nc.vector.memset(plane[:].bitcast(I32), 0)
            return plane

        def load_plane(plane, src, queue, quadrants):
            for q in quadrants:
                queue.dma_start(
                    out=plane[32 * q : 32 * q + 4, :].bitcast(I32),
                    in_=src[0, 4 * q : 4 * q + 4, :].bitcast(I32),
                )

        def load_words(queue, src, width, dtype, name):
            tile = keep.tile([P, width], dtype, name=name, align_bytes=64)
            queue.dma_start(out=tile[:].bitcast(I32), in_=src.bitcast(I32))
            return tile

        tg_rows = tg.rearrange("(p t) q -> p t q", t=PACK)

        def load_gate(t):
            tile = keep.tile([P, Q], F32, name="gate%d" % t, align_bytes=64)
            nc.sync.dma_start(out=tile[:], in_=tg_rows[:, t, :])
            return tile

        xs = zero_plane(T, "xs")
        ws = zero_plane(R, "ws")
        vsc = zero_plane(S, "vsc")
        w2s = zero_plane(R, "w2s")
        tok = load_list(offs, "tok")
        ww = load_words(nc.sync, w_words[0], R, U16, "ww")
        put = load_list(offs2, "put")
        load_plane(xs, xt_scales, nc.sync, range(4))
        xw = load_words(nc.sync, xt_words[0].rearrange("p c b -> p (c b)"), T, U32, "xw")
        load_plane(ws, w_scales, nc.sync, range(4))
        gate = [load_gate(0)]
        look = load_list(offs4, "look")
        slope = keep.tile([P, PACK], F32, name="slope")
        nc.sync.dma_start(out=slope[:], in_=sg.rearrange("(p t) o -> p (t o)", t=PACK))
        shift = keep.tile([P, PACK], F32, name="shift")
        nc.gpsimd.dma_start(out=shift[:], in_=bg.rearrange("(p t) o -> p (t o)", t=PACK))
        w2w = load_words(nc.sync, w2_words[0].rearrange("p c b -> p (c b)"), R, U32, "w2w")
        load_plane(w2s, w2_scales, nc.sync, range(4))
        get = load_list(offs3, "get")
        vw = load_words(nc.sync, vs_words[0], S, U16, "vw")
        entry = load_list(offs5, "entry")
        gate.append(load_gate(1))
        load_plane(vsc, vs_scales, nc.sync, range(4))
        gate.append(load_gate(2))
        gate.append(load_gate(3))

        board = []
        for t in range(PACK):
            tile = keep.tile([P, C], F32, name="board%d" % t, align_bytes=64)
            nc.gpsimd.memset(tile[:], 0.0)
            board.append(tile)

        def deal(copy, src, dtype, name, run):
            dealt = keep.tile([P, PACK, P], dtype, name=name, align_bytes=64)
            copy(
                out=dealt[:].rearrange("p t (g i) -> p g t i", i=run),
                in_=src[:].rearrange("p (g i t) -> p g t i", i=run, t=PACK),
            )
            return dealt

        def pick(src, offsets, dtype, name):
            picked = keep.tile([P, J], dtype, name=name, align_bytes=64)
            nc.vector.tensor_copy(out=picked[:], in_=src[:].indirect(offsets[:]))
            return picked

        xs_g = pick(xs, tok, U8, "xs_g")
        ww_d = deal(nc.scalar.copy, ww, U16, "ww_d", 8)
        xw_g = pick(xw, tok, U32, "xw_g")
        ws_d = deal(nc.vector.tensor_copy, ws, U8, "ws_d", 16)

        sig = keep.tile([P, PACK, J], F32, name="sig", align_bytes=64)

        def look_up_gate(t):
            nc.scalar.activation(
                out=sig[:, t, :], in_=gate[t][:].indirect(look[:]), func=ACT.Sigmoid,
                bias=shift[:, t : t + 1], scale=slope[:, t : t + 1],
            )

        look_up_gate(0)

        a_ps = {}
        for t in (0, 3, 1, 2):
            acc = psum.tile([P, J], F32, name="a_ps%d" % t)
            nc.tensor.matmul_mx(
                out=acc[:], lhsT=ww_d[:, t, :].bitcast(E2M1), lhsT_scale=ws_d[:, t, :],
                rhs=xw_g[:].bitcast(E5M2), rhs_scale=xs_g[:], start=True, stop=True,
            )
            a_ps[t] = acc

        w2w_d = deal(nc.vector.tensor_copy, w2w, U32, "w2w_d", 4)
        w2s_d = deal(nc.vector.tensor_copy, w2s, U8, "w2s_d", 16)
        b_ps = []
        for u in range(2):
            acc = psum.tile([P, 2, J], F32, name="b_ps%d" % u)
            for e in range(2):
                t = 2 * u + e
                nc.tensor.matmul_mx(
                    out=acc[:, e, :], lhsT=w2w_d[:, t, :].bitcast(E4M3), lhsT_scale=w2s_d[:, t, :],
                    rhs=xw_g[:].bitcast(E5M2), rhs_scale=xs_g[:], start=True, stop=True,
                )
            b_ps.append(acc)

        for t in (0, 3, 1, 2):
            a_sb = keep.tile([P, J], F32, name="a_sb%d" % t, align_bytes=64)
            nc.vector.tensor_copy(out=a_sb[:], in_=a_ps[t][:])
            if t < 3:
                nc.scalar.activation(out=board[t][:].indirect(put[:]), in_=a_sb[:], func=ACT.Copy)
            else:
                nc.vector.tensor_copy(out=board[t][:].indirect(put[:]), in_=a_sb[:])

        vw_g = pick(vw, entry, U16, "vw_g")
        vs_g = pick(vsc, entry, U8, "vs_g")

        larger = keep.tile([P, PACK, J], F32, name="larger", align_bytes=64)
        for t in (3, 0, 1, 2):
            got = ring.tile([P, J], F32, name="got", align_bytes=64)
            nc.vector.tensor_copy(out=got[:], in_=board[t][:].indirect(get[:]))
            nc.vector.tensor_tensor(out=larger[:, t, :], in0=got[:], in1=b_ps[t // 2][:, t % 2, :], op=ALU.max)
        for t in range(1, PACK):
            look_up_gate(t)
        halves = [slice(g * P, (g + 1) * P) for g in range(2)]
        hid = keep.tile([P, J, PACK], BF16, name="hid", align_bytes=64)

        def gate_pair(u, slots):
            pair = slice(2 * u, 2 * u + 2)
            nc.vector.tensor_tensor(
                out=hid[:, slots, pair],
                in0=larger[:, pair, slots].rearrange("p t j -> p j t"),
                in1=sig[:, pair, slots].rearrange("p t j -> p j t"),
                op=ALU.mult,
            )

        gate_pair(0, slice(0, J))
        for slots in halves:
            gate_pair(1, slots)
        for g in range(2):
            hid_w = keep.tile([P, P], U32, name="hid_w%d" % g, align_bytes=64)
            hid_s = keep.tile([P, P], U8, name="hid_s%d" % g, align_bytes=64)
            nc.vector.quantize_mx(
                out=hid_w[:].bitcast(E4M3), scales=hid_s[:],
                in_=hid[:, halves[g], :].rearrange("p j t -> p (j t)"),
            )
            for h in range(2):
                acc = psum.tile([P, P], F32, name="a_ps%d" % (2 * g + h))
                nc.tensor.matmul_mx(
                    out=acc[:], lhsT=vw_g[:, halves[h]].bitcast(E2M1), lhsT_scale=vs_g[:, halves[h]],
                    rhs=hid_w[:].bitcast(E4M3), rhs_scale=hid_s[:], start=True, stop=True,
                )
                res = keep.tile([P, P], F32, name="res%d" % (2 * g + h), align_bytes=64)
                last = g == 1 and h == 1
                if last:
                    nc.vector.tensor_copy(out=res[:], in_=acc[:])
                else:
                    nc.scalar.copy(out=res[:], in_=acc[:])
                queue = nc.scalar if (g == 1 and h == 0) else nc.sync
                queue.dma_start(out=out[halves[h], halves[g]], in_=res[:])
